import numpy as np
import ml_dtypes


def mxq(x, axis, fmt="e4m3"):
    dtype, down = {"e4m3": (ml_dtypes.float8_e4m3fn, 7), "e5m2": (ml_dtypes.float8_e5m2, 14)}[fmt]
    v = np.moveaxis(np.asarray(x, np.float32).astype(ml_dtypes.bfloat16).astype(np.float64), axis, -1)
    blocks = v.reshape(v.shape[:-1] + (-1, 32))
    amax = np.abs(blocks).max(-1, keepdims=True)
    byte = np.maximum(np.where(amax > 0, np.frexp(amax)[1] - 1 + 127, 0) - down, 1)
    scale = np.exp2(byte - 127.0)
    codes = (blocks / scale).astype(np.float32).astype(dtype).astype(np.float64)
    return np.moveaxis((codes * scale).reshape(v.shape), -1, axis)


WIDE = False


def mx_kscale(k):
    if not WIDE:
        return np.ones(k)
    levels = np.array([10, -10, 5, -5, 0])
    if k % 512:
        return np.exp2(np.random.permutation(np.resize(levels, k // 32))).repeat(32)
    a = np.empty((k // 512, 16))
    for p in range(k // 512):
        a[p, :8] = np.random.permutation(np.resize(levels, 8))
        for g in range(8):
            far = levels[np.abs(levels - a[p, g]) >= 10]
            a[p, g + 8] = far[np.random.randint(len(far))]
    return np.exp2(a.ravel()).repeat(32)


def f64(x):
    return np.asarray(x).astype(np.float64)


def striped(idx):
    return np.tile(np.asarray(idx).reshape(-1, 16).T, (8, 1)).astype(np.uint16)


def unstriped(offs):
    return offs[:16].T.reshape(-1).astype(np.int64)


B, N, T, D, DV, NQ = 2, 512, 2048, 512, 256, 128
PAGE = 64
DRAFT = 128


def setup_inputs():
    n = np.random.standard_normal
    pages = np.random.permutation(T // PAGE)[:B * N // PAGE]
    idx = (pages[:, None] * PAGE + np.arange(PAGE)[None, :]).reshape(-1)
    s = mx_kscale(D)[:, None]
    u = np.ones(T)
    u[idx] = mx_kscale(B * N)
    r = np.random.uniform(0.5, 2.0, T)
    rk = np.random.uniform(0.5, 2.0, T)
    k = n((D, T)) / s / rk
    v = n((DV, T)) / (u * r)
    when = np.zeros(T)
    when[idx] = np.concatenate([np.concatenate([np.arange(N - DRAFT), N - DRAFT + np.random.randint(0, 16, DRAFT)]) for b in range(B)])
    return {
        "qT": (n((B, D, NQ)) * s * (0.80 / np.sqrt(D))).astype(np.float32),
        "kT": k.astype(np.float32),
        "vT": v.astype(np.float32),
        "ks": np.tile(rk, (128, 1)).astype(np.float32),
        "vs": np.tile(u * r, (128, 1)).astype(np.float32),
        "pos": np.tile(when, (128, 1)).astype(np.float32),
        "qpos": np.random.randint(N - DRAFT, N - DRAFT + 16, (B, NQ, 1)).astype(np.float32),
        "offs": striped(idx),
    }


def reference(qT, kT, vT, ks, vs, pos, qpos, offs):
    idx = unstriped(offs)
    k = f64(kT)
    v = f64(vT)
    pick = lambda x: x[:, idx].reshape(x.shape[0], B, N).transpose(1, 0, 2)
    q = f64(qT)
    score = mxq(q, 1, "e4m3").transpose(0, 2, 1) @ mxq(pick(k), 1, "e4m3")
    score = score * pick(f64(ks))[:, :1, :]
    score = np.where(pick(f64(pos))[:, :1, :] <= f64(qpos), score, -30000.0)
    m = score.max(-1, keepdims=True)
    p = np.exp(score - m)
    total = p.sum(-1, keepdims=True)
    w = p * pick(f64(vs))[:, :1, :]
    y = mxq(w, 2, "e4m3") @ mxq(pick(v).transpose(0, 2, 1), 1, "e4m3")
    y = y / total
    return y

@@ -1,0 +1,241 @@
+from contextlib import ExitStack
+
+import concourse.mybir as mybir
+from concourse.masks import make_identity
+
+F32 = mybir.dt.float32
+BF16 = mybir.dt.bfloat16
+U32 = mybir.dt.uint32
+U16 = mybir.dt.uint16
+U8 = mybir.dt.uint8
+FP8X4 = mybir.dt.float8_e4m3fn_x4
+ALU = mybir.AluOpType
+ACT = mybir.ActivationFunctionType
+AXIS_X = mybir.AxisListType.X
+
+B, NQ, D, DV, N, T = 2, 128, 512, 256, 512, 2048
+P = 128
+PACK = 4
+E_BLOCKS = DV // P
+MASKED = 30000.0
+VECTOR_COLS = 320
+
+FLOPS = 2 * B * NQ * N * (D + DV)
+BYTES = 4 * (B * D * NQ + (D + DV) * T + 3 * T + B * NQ + B * NQ * DV) + 2 * P * (B * N // 16)
+
+
+def tile_attend_x_ks_draft_kernel(tc, qT, kT, vT, ks, vs, pos, qpos, offs, out):
+    nc = tc.nc
+    with ExitStack() as ctx:
+        keep = ctx.enter_context(tc.tile_pool(name="keep", bufs=1))
+        psum = ctx.enter_context(tc.psum_pool(name="psum", bufs=8))
+
+        def bank():
+            return psum.tile([P, 512], F32, name="bank")
+
+        offsets = keep.tile([P, B * N // 16], U16, name="offsets")
+        nc.sync.dma_start(offsets[:], offs)
+        rows = {}
+        for name, src in (("pos", pos), ("ks", ks), ("vs", vs)):
+            rows[name] = keep.tile([P, T // P], F32, name=name + "_row")
+            nc.scalar.dma_start(rows[name][:], src[0:1, :].rearrange("o (n j) -> (o n) j", j=T // P))
+        q_place = []
+        for s in range(B):
+            q_place.append(keep.tile([P, 1], F32, name=f"q_place{s}"))
+            nc.scalar.dma_start(q_place[s][:], qpos[s])
+        k_rows = kT.rearrange("(p t) n -> p t n", t=PACK)
+        k_pool = [keep.tile([P, T], F32, name=f"k_pool{t}") for t in range(PACK)]
+        v_pool = [keep.tile([P, T], F32, name=f"v_pool{e}") for e in range(E_BLOCKS)]
+        q_raw = keep.tile([P, B, PACK, NQ], F32, name="q_raw")
+        nc.sync.dma_start(k_pool[0][:], k_rows[:, 0, :])
+        nc.sync.dma_start(k_pool[1][:], k_rows[:, 1, :])
+        nc.sync.dma_start(q_raw[:], qT.rearrange("b (p t) q -> p b t q", t=PACK))
+        nc.sync.dma_start(k_pool[2][:], k_rows[:, 2, :])
+        nc.sync.dma_start(k_pool[3][:], k_rows[:, 3, :])
+        for e in range(E_BLOCKS):
+            nc.sync.dma_start(v_pool[e][:], vT[e * P : (e + 1) * P, :])
+
+        ident = keep.tile([P, P], F32, name="ident")
+        make_identity(nc, ident[:])
+        warm = keep.tile([P, 1], F32, name="warm")
+        nc.vector.memset(warm[:], 0.0)
+        nc.scalar.activation(warm[:], warm[:], ACT.Exp)
+
+        def table(name):
+            wide = keep.tile([P, T], F32, name=name + "_table")
+            cols = wide[:].rearrange("p (n j) -> p n j", j=T // P)
+            for b in range(4):
+                ps = bank()
+                for i in range(4):
+                    j = 4 * b + i
+                    nc.tensor.transpose(ps[:, i * P : (i + 1) * P], rows[name][:, j : j + 1].to_broadcast([P, P]), ident[:])
+                nc.scalar.copy(out=cols[:, :, 4 * b : 4 * b + 4], in_=ps[:].rearrange("p (i n) -> p n i", i=4))
+            return wide
+
+        pos_table = table("pos")
+        ks_table = table("ks")
+
+        k_got = keep.tile([P, PACK, B * N], F32, name="k_got")
+        nc.vector.tensor_copy(k_got[:, 0, :], k_pool[0][:].indirect(offsets[:]))
+
+        def seq(s):
+            return slice(s * N, (s + 1) * N)
+
+        def seq_offsets(s):
+            return offsets[:, s * (N // 16) : (s + 1) * (N // 16)]
+
+        pos_got = keep.tile([P, B * N], F32, name="pos_got")
+        nc.vector.tensor_copy(pos_got[:], pos_table[:].indirect(offsets[:]))
+        negmask = keep.tile([P, B * N], F32, name="negmask")
+        for s in range(B):
+            nc.vector.tensor_scalar(negmask[:, seq(s)], pos_got[:, seq(s)], q_place[s][:], -1.0, ALU.is_le, ALU.mult)
+        floor = keep.tile([P, B * N], F32, name="floor")
+        nc.vector.tensor_scalar(floor[:], negmask[:], 1.0, MASKED, ALU.add, ALU.mult)
+        nks = keep.tile([P, B * N], F32, name="nks")
+        nc.vector.tensor_copy(k_got[:, 1, :], k_pool[1][:].indirect(offsets[:]))
+        for s in range(B):
+            nc.vector.tensor_tensor(nks[:, seq(s)], ks_table[:].indirect(seq_offsets(s)), negmask[:, seq(s)], ALU.mult)
+
+        q_bf = keep.tile([P, B, NQ, PACK], BF16, name="q_bf", align_bytes=64)
+        nc.scalar.copy(out=q_bf[:], in_=q_raw[:].rearrange("p b t q -> p b q t"))
+        q_codes = keep.tile([P, B * NQ], U32, name="q_codes", align_bytes=64)
+        q_scales = keep.tile([P, B * NQ], U8, name="q_scales", align_bytes=64)
+        nc.vector.quantize_mx(
+            out=q_codes[:].bitcast(FP8X4), scales=q_scales[:], in_=q_bf[:].rearrange("p b q t -> p (b q t)")
+        )
+        nc.vector.tensor_copy(k_got[:, 2, :], k_pool[2][:].indirect(offsets[:]))
+
+        vs_table = table("vs")
+        vs_got = keep.tile([P, B * N], F32, name="vs_got")
+        nc.vector.tensor_copy(vs_got[:], vs_table[:].indirect(offsets[:]))
+        vs_slot = keep.tile([P, B * PACK], F32, name="vs_slot")
+        for s in range(B):
+            ps = bank()
+            for t in range(PACK):
+                nc.tensor.transpose(ps[:, t * P : (t + 1) * P], vs_got[:, s * N + t : (s + 1) * N : PACK], ident[:])
+            nc.scalar.copy(out=vs_slot[:, s * PACK : (s + 1) * PACK], in_=ps[:, 0 : 512 : P])
+
+        k_bf = [keep.tile([P, N, PACK], BF16, name=f"k_bf{s}", align_bytes=64) for s in range(B)]
+        k_codes = [keep.tile([P, N], U32, name=f"k_codes{s}", align_bytes=64) for s in range(B)]
+        k_scales = [keep.tile([P, N], U8, name=f"k_scales{s}", align_bytes=64) for s in range(B)]
+
+        def gather_k3(s):
+            nc.vector.tensor_copy(k_got[:, 3, seq(s)], k_pool[3][:].indirect(seq_offsets(s)))
+
+        def interleave(copy, s, a, z):
+            copy(out=k_bf[s][:, a:z, :], in_=k_got[:, :, s * N + a : s * N + z].rearrange("p t n -> p n t"))
+
+        def quantize_k(s):
+            nc.vector.quantize_mx(
+                out=k_codes[s][:].bitcast(FP8X4), scales=k_scales[s][:], in_=k_bf[s][:].rearrange("p n t -> p (n t)")
+            )
+
+        score = [None, None]
+
+        def scores(s):
+            score[s] = bank()
+            qc = slice(s * NQ, (s + 1) * NQ)
+            nc.tensor.matmul_mx(
+                out=score[s][:], lhsT=q_codes[:, qc].bitcast(FP8X4), lhsT_scale=q_scales[:, qc],
+                rhs=k_codes[s][:].bitcast(FP8X4), rhs_scale=k_scales[s][:], start=True, stop=True,
+            )
+
+        scaled = [keep.tile([P, N], F32, name=f"scaled{s}") for s in range(B)]
+        masked = [keep.tile([P, N], F32, name=f"masked{s}") for s in range(B)]
+        negmax = [keep.tile([P, 1], F32, name=f"negmax{s}") for s in range(B)]
+        total = [keep.tile([P, 1], F32, name=f"total{s}") for s in range(B)]
+        inv = [keep.tile([P, 1], F32, name=f"inv{s}") for s in range(B)]
+        prob = [keep.tile([P, PACK, P], F32, name=f"prob{s}") for s in range(B)]
+        w_bf = [keep.tile([P, NQ, PACK], BF16, name=f"w_bf{s}", align_bytes=64) for s in range(B)]
+        w_codes = [keep.tile([P, NQ], U32, name=f"w_codes{s}", align_bytes=64) for s in range(B)]
+        w_scales = [keep.tile([P, NQ], U8, name=f"w_scales{s}", align_bytes=64) for s in range(B)]
+        v_got = [keep.tile([P, B * N], F32, name=f"v_got{e}") for e in range(E_BLOCKS)]
+        v_bf = [keep.tile([P, DV, PACK], BF16, name=f"v_bf{s}", align_bytes=64) for s in range(B)]
+        v_codes = [keep.tile([P, DV], U32, name=f"v_codes{s}", align_bytes=64) for s in range(B)]
+        v_scales = [keep.tile([P, DV], U8, name=f"v_scales{s}", align_bytes=64) for s in range(B)]
+        result = [keep.tile([P, DV], F32, name=f"result{s}") for s in range(B)]
+
+        def scale_scores(s):
+            nc.vector.tensor_tensor(scaled[s][:], score[s][:], nks[:, seq(s)], ALU.mult)
+
+        def mask_scores(s):
+            nc.vector.tensor_tensor(masked[s][:], scaled[s][:], floor[:, seq(s)], ALU.add)
+
+        def row_max(s):
+            nc.vector.tensor_reduce(negmax[s][:], masked[s][:], AXIS_X, ALU.min)
+
+        def exponent(s):
+            nc.scalar.activation(
+                prob[s][:], masked[s][:].rearrange("q (i t) -> q t i", t=PACK), ACT.Exp,
+                bias=negmax[s][:], scale=-1.0, accum_out=total[s][:],
+            )
+
+        def weights(s):
+            ps = bank()
+            for t in range(PACK):
+                nc.tensor.transpose(ps[:, t * P : (t + 1) * P], prob[s][:, t, :], ident[:])
+            nc.vector.tensor_tensor(
+                w_bf[s][:], ps[:].rearrange("p (t q) -> p q t", t=PACK),
+                vs_slot[:, s * PACK : (s + 1) * PACK].unsqueeze(1).to_broadcast([P, NQ, PACK]), ALU.mult,
+            )
+
+        def quantize_w(s):
+            nc.vector.quantize_mx(
+                out=w_codes[s][:].bitcast(FP8X4), scales=w_scales[s][:], in_=w_bf[s][:].rearrange("p q t -> p (q t)")
+            )
+
+        def gather_v(e):
+            nc.vector.tensor_copy(v_got[e][:], v_pool[e][:].indirect(offsets[:]))
+
+        def turn_v(e):
+            for s in range(B):
+                ps = bank()
+                for t in range(PACK):
+                    nc.tensor.transpose(ps[:, t * P : (t + 1) * P], v_got[e][:, s * N + t : (s + 1) * N : PACK], ident[:])
+                nc.scalar.copy(out=v_bf[s][:, e * P : (e + 1) * P, :], in_=ps[:].rearrange("p (t c) -> p c t", t=PACK))
+
+        def quantize_v(s):
+            nc.vector.quantize_mx(
+                out=v_codes[s][:].bitcast(FP8X4), scales=v_scales[s][:], in_=v_bf[s][:].rearrange("p c t -> p (c t)")
+            )
+
+        def values(s):
+            ps = bank()
+            nc.tensor.matmul_mx(
+                out=ps[:, 0:DV], lhsT=w_codes[s][:].bitcast(FP8X4), lhsT_scale=w_scales[s][:],
+                rhs=v_codes[s][:].bitcast(FP8X4), rhs_scale=v_scales[s][:], start=True, stop=True,
+            )
+            nc.scalar.activation(result[s][:], ps[:, 0:DV], ACT.Copy, scale=inv[s][:])
+            nc.sync.dma_start(out[s], result[s][:])
+
+        gather_k3(0)
+        interleave(nc.scalar.copy, 0, VECTOR_COLS, N)
+        interleave(nc.vector.tensor_copy, 0, 0, VECTOR_COLS)
+        gather_k3(1)
+        interleave(nc.scalar.copy, 1, 0, N)
+        quantize_k(0)
+        scores(0)
+        gather_v(0)
+        turn_v(0)
+        scale_scores(0)
+        quantize_k(1)
+        scores(1)
+        gather_v(1)
+        mask_scores(0)
+        row_max(0)
+        exponent(0)
+        turn_v(1)
+        scale_scores(1)
+        mask_scores(1)
+        row_max(1)
+        exponent(1)
+        weights(0)
+        quantize_v(0)
+        quantize_w(0)
+        nc.vector.reciprocal(inv[0][:], total[0][:])
+        values(0)
+        weights(1)
+        quantize_v(1)
+        quantize_w(1)
+        nc.vector.reciprocal(inv[1][:], total[1][:])
+        values(1)

@@ -16,9 +16,10 @@ AXIS_X = mybir.AxisListType.X
 B, NQ, D, DV, N, T = 2, 128, 512, 256, 512, 2048
 P = 128
 PACK = 4
+CHUNKS = N // P
 E_BLOCKS = DV // P
-MASKED = 30000.0
-VECTOR_COLS = 320
+MASKED = 1.0e30
+VECTOR_COLS = 256
 
 FLOPS = 2 * B * NQ * N * (D + DV)
 BYTES = 4 * (B * D * NQ + (D + DV) * T + 3 * T + B * NQ + B * NQ * DV) + 2 * P * (B * N // 16)
@@ -33,15 +34,21 @@ def tile_attend_x_ks_draft_kernel(tc, qT, kT, vT, ks, vs, pos, qpos, offs, out):
         def bank():
             return psum.tile([P, 512], F32, name="bank")
 
+        def per_seq(shape, dtype, name, align=32):
+            return [keep.tile(shape, dtype, name=f"{name}{s}", align_bytes=align) for s in range(B)]
+
+        def seq(s):
+            return slice(s * N, (s + 1) * N)
+
         offsets = keep.tile([P, B * N // 16], U16, name="offsets")
         nc.sync.dma_start(offsets[:], offs)
-        rows = {}
-        for name, src in (("pos", pos), ("ks", ks), ("vs", vs)):
-            rows[name] = keep.tile([P, T // P], F32, name=name + "_row")
-            nc.scalar.dma_start(rows[name][:], src[0:1, :].rearrange("o (n j) -> (o n) j", j=T // P))
-        q_place = []
+        table = {}
+        for name, src, engine in (("pos", pos, nc.vector), ("ks", ks, nc.gpsimd), ("vs", vs, nc.vector)):
+            table[name] = keep.tile([P, T], F32, name=name + "_table")
+            engine.memset(table[name][:], 0.0)
+            nc.scalar.dma_start(table[name][0:1, :], src[0:1, :])
+        q_place = per_seq([P, 1], F32, "q_place")
         for s in range(B):
-            q_place.append(keep.tile([P, 1], F32, name=f"q_place{s}"))
             nc.scalar.dma_start(q_place[s][:], qpos[s])
         k_rows = kT.rearrange("(p t) n -> p t n", t=PACK)
         k_pool = [keep.tile([P, T], F32, name=f"k_pool{t}") for t in range(PACK)]
@@ -61,40 +68,59 @@ def tile_attend_x_ks_draft_kernel(tc, qT, kT, vT, ks, vs, pos, qpos, offs, out):
         nc.vector.memset(warm[:], 0.0)
         nc.scalar.activation(warm[:], warm[:], ACT.Exp)
 
-        def table(name):
-            wide = keep.tile([P, T], F32, name=name + "_table")
-            cols = wide[:].rearrange("p (n j) -> p n j", j=T // P)
-            for b in range(4):
-                ps = bank()
-                for i in range(4):
-                    j = 4 * b + i
-                    nc.tensor.transpose(ps[:, i * P : (i + 1) * P], rows[name][:, j : j + 1].to_broadcast([P, P]), ident[:])
-                nc.scalar.copy(out=cols[:, :, 4 * b : 4 * b + 4], in_=ps[:].rearrange("p (i n) -> p n i", i=4))
-            return wide
+        q_row = keep.tile([P, B, NQ], F32, name="q_row")
+        ps = bank()
+        for s in range(B):
+            nc.tensor.transpose(ps[:, s * NQ : (s + 1) * NQ], q_place[s][:].to_broadcast([P, P]), ident[:])
+        nc.scalar.copy(out=q_row[:].rearrange("p b q -> p (b q)"), in_=ps[:, 0 : B * NQ])
 
-        pos_table = table("pos")
-        ks_table = table("ks")
+        def gather_table(name):
+            got = keep.tile([P, B * N], F32, name=name + "_got")
+            nc.vector.tensor_copy(got[:], table[name][:].indirect(offsets[:]))
+            return got
+
+        def turn_table(name, got, start, step, scale):
+            col = per_seq([P, CHUNKS], F32, name + "_col")
+            for s in range(B):
+                ps = bank()
+                for c in range(CHUNKS):
+                    a = s * N + c * start
+                    nc.tensor.transpose(ps[:, c * P : (c + 1) * P], got[:, a : a + (P - 1) * step + 1 : step], ident[:])
+                nc.scalar.activation(col[s][:], ps[:, 0 : 512 : P], ACT.Copy, scale=scale)
+            return col
+
+        pos_col = turn_table("pos", gather_table("pos"), P, 1, 1.0)
+        limit = per_seq([P, CHUNKS, NQ], F32, "limit")
+        for s in range(B):
+            for c in range(CHUNKS):
+                nc.gpsimd.tensor_scalar(
+                    limit[s][:, c, :], q_row[:, s, :], pos_col[s][:, c : c + 1], MASKED, ALU.is_lt, ALU.mult
+                )
+        nks_col = turn_table("ks", gather_table("ks"), P, 1, -1.0)
 
         k_got = keep.tile([P, PACK, B * N], F32, name="k_got")
-        nc.vector.tensor_copy(k_got[:, 0, :], k_pool[0][:].indirect(offsets[:]))
+        k_bf = per_seq([P, N, PACK], BF16, "k_bf", 64)
+        k_codes = per_seq([P, N], U32, "k_codes", 64)
+        k_scales = per_seq([P, N], U8, "k_scales", 64)
 
-        def seq(s):
-            return slice(s * N, (s + 1) * N)
+        def gather_k(t):
+            nc.vector.tensor_copy(k_got[:, t, :], k_pool[t][:].indirect(offsets[:]))
 
-        def seq_offsets(s):
-            return offsets[:, s * (N // 16) : (s + 1) * (N // 16)]
+        def gather_last_k(s):
+            list_s = offsets[:, s * (N // 16) : (s + 1) * (N // 16)]
+            nc.vector.tensor_copy(k_got[:, 3, seq(s)], k_pool[3][:].indirect(list_s))
 
-        pos_got = keep.tile([P, B * N], F32, name="pos_got")
-        nc.vector.tensor_copy(pos_got[:], pos_table[:].indirect(offsets[:]))
-        negmask = keep.tile([P, B * N], F32, name="negmask")
-        for s in range(B):
-            nc.vector.tensor_scalar(negmask[:, seq(s)], pos_got[:, seq(s)], q_place[s][:], -1.0, ALU.is_le, ALU.mult)
-        floor = keep.tile([P, B * N], F32, name="floor")
-        nc.vector.tensor_scalar(floor[:], negmask[:], 1.0, MASKED, ALU.add, ALU.mult)
-        nks = keep.tile([P, B * N], F32, name="nks")
-        nc.vector.tensor_copy(k_got[:, 1, :], k_pool[1][:].indirect(offsets[:]))
-        for s in range(B):
-            nc.vector.tensor_tensor(nks[:, seq(s)], ks_table[:].indirect(seq_offsets(s)), negmask[:, seq(s)], ALU.mult)
+        def interleave(copy, s, t, a, z):
+            copy(out=k_bf[s][:, a:z, t : t + 2], in_=k_got[:, t : t + 2, s * N + a : s * N + z].rearrange("p t n -> p n t"))
+
+        def quantize_k(s):
+            nc.vector.quantize_mx(
+                out=k_codes[s][:].bitcast(FP8X4), scales=k_scales[s][:], in_=k_bf[s][:].rearrange("p n t -> p (n t)")
+            )
+
+        gather_k(0)
+        vs_col = turn_table("vs", gather_table("vs"), 1, PACK, 1.0)
+        gather_k(1)
 
         q_bf = keep.tile([P, B, NQ, PACK], BF16, name="q_bf", align_bytes=64)
         nc.scalar.copy(out=q_bf[:], in_=q_raw[:].rearrange("p b t q -> p b q t"))
@@ -103,80 +129,70 @@ def tile_attend_x_ks_draft_kernel(tc, qT, kT, vT, ks, vs, pos, qpos, offs, out):
         nc.vector.quantize_mx(
             out=q_codes[:].bitcast(FP8X4), scales=q_scales[:], in_=q_bf[:].rearrange("p b q t -> p (b q t)")
         )
-        nc.vector.tensor_copy(k_got[:, 2, :], k_pool[2][:].indirect(offsets[:]))
-
-        vs_table = table("vs")
-        vs_got = keep.tile([P, B * N], F32, name="vs_got")
-        nc.vector.tensor_copy(vs_got[:], vs_table[:].indirect(offsets[:]))
-        vs_slot = keep.tile([P, B * PACK], F32, name="vs_slot")
         for s in range(B):
-            ps = bank()
-            for t in range(PACK):
-                nc.tensor.transpose(ps[:, t * P : (t + 1) * P], vs_got[:, s * N + t : (s + 1) * N : PACK], ident[:])
-            nc.scalar.copy(out=vs_slot[:, s * PACK : (s + 1) * PACK], in_=ps[:, 0 : 512 : P])
+            interleave(nc.scalar.copy, s, 0, 0, N)
+        gather_k(2)
 
-        k_bf = [keep.tile([P, N, PACK], BF16, name=f"k_bf{s}", align_bytes=64) for s in range(B)]
-        k_codes = [keep.tile([P, N], U32, name=f"k_codes{s}", align_bytes=64) for s in range(B)]
-        k_scales = [keep.tile([P, N], U8, name=f"k_scales{s}", align_bytes=64) for s in range(B)]
-
-        def gather_k3(s):
-            nc.vector.tensor_copy(k_got[:, 3, seq(s)], k_pool[3][:].indirect(seq_offsets(s)))
-
-        def interleave(copy, s, a, z):
-            copy(out=k_bf[s][:, a:z, :], in_=k_got[:, :, s * N + a : s * N + z].rearrange("p t n -> p n t"))
-
-        def quantize_k(s):
-            nc.vector.quantize_mx(
-                out=k_codes[s][:].bitcast(FP8X4), scales=k_scales[s][:], in_=k_bf[s][:].rearrange("p n t -> p (n t)")
-            )
-
-        score = [None, None]
+        scaled = per_seq([P, CHUNKS, NQ], F32, "scaled")
+        negmax = per_seq([P, 1], F32, "negmax")
+        total = per_seq([P, 1], F32, "total")
+        inv = per_seq([P, 1], F32, "inv")
+        prob = per_seq([P, PACK, P], F32, "prob")
+        w_bf = per_seq([P, NQ, PACK], BF16, "w_bf", 64)
+        w_codes = per_seq([P, NQ], U32, "w_codes", 64)
+        w_scales = per_seq([P, NQ], U8, "w_scales", 64)
+        v_got = [keep.tile([P, B * N], F32, name=f"v_got{e}") for e in range(E_BLOCKS)]
+        v_bf = per_seq([P, DV, PACK], BF16, "v_bf", 64)
+        v_codes = per_seq([P, DV], U32, "v_codes", 64)
+        v_scales = per_seq([P, DV], U8, "v_scales", 64)
+        result = per_seq([P, DV], F32, "result")
+        turned = {}
 
         def scores(s):
-            score[s] = bank()
+            ps = bank()
             qc = slice(s * NQ, (s + 1) * NQ)
-            nc.tensor.matmul_mx(
-                out=score[s][:], lhsT=q_codes[:, qc].bitcast(FP8X4), lhsT_scale=q_scales[:, qc],
-                rhs=k_codes[s][:].bitcast(FP8X4), rhs_scale=k_scales[s][:], start=True, stop=True,
-            )
+            for c in range(CHUNKS):
+                kc = slice(c * P, (c + 1) * P)
+                nc.tensor.matmul_mx(
+                    out=ps[:, kc], lhsT=k_codes[s][:, kc].bitcast(FP8X4), lhsT_scale=k_scales[s][:, kc],
+                    rhs=q_codes[:, qc].bitcast(FP8X4), rhs_scale=q_scales[:, qc], start=True, stop=True,
+                )
+            turned["raw", s] = ps
 
-        scaled = [keep.tile([P, N], F32, name=f"scaled{s}") for s in range(B)]
-        masked = [keep.tile([P, N], F32, name=f"masked{s}") for s in range(B)]
-        negmax = [keep.tile([P, 1], F32, name=f"negmax{s}") for s in range(B)]
-        total = [keep.tile([P, 1], F32, name=f"total{s}") for s in range(B)]
-        inv = [keep.tile([P, 1], F32, name=f"inv{s}") for s in range(B)]
-        prob = [keep.tile([P, PACK, P], F32, name=f"prob{s}") for s in range(B)]
-        w_bf = [keep.tile([P, NQ, PACK], BF16, name=f"w_bf{s}", align_bytes=64) for s in range(B)]
-        w_codes = [keep.tile([P, NQ], U32, name=f"w_codes{s}", align_bytes=64) for s in range(B)]
-        w_scales = [keep.tile([P, NQ], U8, name=f"w_scales{s}", align_bytes=64) for s in range(B)]
-        v_got = [keep.tile([P, B * N], F32, name=f"v_got{e}") for e in range(E_BLOCKS)]
-        v_bf = [keep.tile([P, DV, PACK], BF16, name=f"v_bf{s}", align_bytes=64) for s in range(B)]
-        v_codes = [keep.tile([P, DV], U32, name=f"v_codes{s}", align_bytes=64) for s in range(B)]
-        v_scales = [keep.tile([P, DV], U8, name=f"v_scales{s}", align_bytes=64) for s in range(B)]
-        result = [keep.tile([P, DV], F32, name=f"result{s}") for s in range(B)]
+        def scale_and_mask(s):
+            ps = turned["raw", s]
+            for c in range(CHUNKS):
+                nc.scalar.activation(
+                    scaled[s][:, c, :], ps[:, c * P : (c + 1) * P], ACT.Copy, scale=nks_col[s][:, c : c + 1]
+                )
 
-        def scale_scores(s):
-            nc.vector.tensor_tensor(scaled[s][:], score[s][:], nks[:, seq(s)], ALU.mult)
-
-        def mask_scores(s):
-            nc.vector.tensor_tensor(masked[s][:], scaled[s][:], floor[:, seq(s)], ALU.add)
+        def turn_scores(s):
+            ps = bank()
+            for c in range(CHUNKS):
+                kc = slice(c * P, (c + 1) * P)
+                nc.tensor.matmul(ps[:, kc], limit[s][:, c, :], ident[:], is_transpose=True, start=True, stop=False)
+                nc.tensor.matmul(ps[:, kc], scaled[s][:, c, :], ident[:], is_transpose=True, start=False, stop=True)
+            turned["score", s] = ps
 
         def row_max(s):
-            nc.vector.tensor_reduce(negmax[s][:], masked[s][:], AXIS_X, ALU.min)
+            nc.vector.tensor_reduce(negmax[s][:], turned["score", s][:], AXIS_X, ALU.min)
 
         def exponent(s):
             nc.scalar.activation(
-                prob[s][:], masked[s][:].rearrange("q (i t) -> q t i", t=PACK), ACT.Exp,
-                bias=negmax[s][:], scale=-1.0, accum_out=total[s][:],
+                prob[s][:].rearrange("q t i -> q i t"), turned["score", s][:].rearrange("q (i t) -> q i t", t=PACK),
+                ACT.Exp, bias=negmax[s][:], scale=-1.0, accum_out=total[s][:],
             )
 
-        def weights(s):
+        def turn_prob(s):
             ps = bank()
             for t in range(PACK):
                 nc.tensor.transpose(ps[:, t * P : (t + 1) * P], prob[s][:, t, :], ident[:])
+            turned["prob", s] = ps
+
+        def weights(s):
             nc.vector.tensor_tensor(
-                w_bf[s][:], ps[:].rearrange("p (t q) -> p q t", t=PACK),
-                vs_slot[:, s * PACK : (s + 1) * PACK].unsqueeze(1).to_broadcast([P, NQ, PACK]), ALU.mult,
+                w_bf[s][:], turned["prob", s][:].rearrange("p (t q) -> p q t", t=PACK),
+                vs_col[s][:].unsqueeze(1).to_broadcast([P, NQ, PACK]), ALU.mult,
             )
 
         def quantize_w(s):
@@ -187,12 +203,11 @@ def tile_attend_x_ks_draft_kernel(tc, qT, kT, vT, ks, vs, pos, qpos, offs, out):
         def gather_v(e):
             nc.vector.tensor_copy(v_got[e][:], v_pool[e][:].indirect(offsets[:]))
 
-        def turn_v(e):
-            for s in range(B):
-                ps = bank()
-                for t in range(PACK):
-                    nc.tensor.transpose(ps[:, t * P : (t + 1) * P], v_got[e][:, s * N + t : (s + 1) * N : PACK], ident[:])
-                nc.scalar.copy(out=v_bf[s][:, e * P : (e + 1) * P, :], in_=ps[:].rearrange("p (t c) -> p c t", t=PACK))
+        def turn_v(e, s):
+            ps = bank()
+            for t in range(PACK):
+                nc.tensor.transpose(ps[:, t * P : (t + 1) * P], v_got[e][:, s * N + t : (s + 1) * N : PACK], ident[:])
+            nc.scalar.copy(out=v_bf[s][:, e * P : (e + 1) * P, :], in_=ps[:].rearrange("p (t c) -> p c t", t=PACK))
 
         def quantize_v(s):
             nc.vector.quantize_mx(
@@ -208,34 +223,39 @@ def tile_attend_x_ks_draft_kernel(tc, qT, kT, vT, ks, vs, pos, qpos, offs, out):
             nc.scalar.activation(result[s][:], ps[:, 0:DV], ACT.Copy, scale=inv[s][:])
             nc.sync.dma_start(out[s], result[s][:])
 
-        gather_k3(0)
-        interleave(nc.scalar.copy, 0, VECTOR_COLS, N)
-        interleave(nc.vector.tensor_copy, 0, 0, VECTOR_COLS)
-        gather_k3(1)
-        interleave(nc.scalar.copy, 1, 0, N)
+        gather_last_k(0)
+        interleave(nc.scalar.copy, 0, 2, VECTOR_COLS, N)
+        gather_last_k(1)
+        interleave(nc.vector.tensor_copy, 0, 2, 0, VECTOR_COLS)
+        interleave(nc.scalar.copy, 1, 2, VECTOR_COLS, N)
+        interleave(nc.vector.tensor_copy, 1, 2, 0, VECTOR_COLS)
         quantize_k(0)
-        scores(0)
-        gather_v(0)
-        turn_v(0)
-        scale_scores(0)
         quantize_k(1)
+        scores(0)
         scores(1)
+        gather_v(0)
+        scale_and_mask(0)
+        scale_and_mask(1)
+        turn_scores(0)
+        turn_scores(1)
         gather_v(1)
-        mask_scores(0)
         row_max(0)
-        exponent(0)
-        turn_v(1)
-        scale_scores(1)
-        mask_scores(1)
         row_max(1)
+        turn_v(0, 0)
+        turn_v(0, 1)
+        exponent(0)
         exponent(1)
+        turn_prob(0)
         weights(0)
-        quantize_v(0)
+        turn_v(1, 0)
+        turn_v(1, 1)
+        turn_prob(1)
         quantize_w(0)
-        nc.vector.reciprocal(inv[0][:], total[0][:])
-        values(0)
         weights(1)
-        quantize_v(1)
-        quantize_w(1)
+        nc.vector.reciprocal(inv[0][:], total[0][:])
         nc.vector.reciprocal(inv[1][:], total[1][:])
+        quantize_v(0)
+        values(0)
+        quantize_w(1)
+        quantize_v(1)
         values(1)

@@ -91,11 +91,13 @@ def tile_attend_x_ks_draft_kernel(tc, qT, kT, vT, ks, vs, pos, qpos, offs, out):
 
         pos_col = turn_table("pos", gather_table("pos"), P, 1, 1.0)
         limit = per_seq([P, CHUNKS, NQ], F32, "limit")
-        for s in range(B):
+
+        def mask(s):
             for c in range(CHUNKS):
-                nc.gpsimd.tensor_scalar(
+                nc.vector.tensor_scalar(
                     limit[s][:, c, :], q_row[:, s, :], pos_col[s][:, c : c + 1], MASKED, ALU.is_lt, ALU.mult
                 )
+
         nks_col = turn_table("ks", gather_table("ks"), P, 1, -1.0)
 
         k_got = keep.tile([P, PACK, B * N], F32, name="k_got")
@@ -233,6 +235,8 @@ def tile_attend_x_ks_draft_kernel(tc, qT, kT, vT, ks, vs, pos, qpos, offs, out):
         quantize_k(1)
         scores(0)
         scores(1)
+        mask(0)
+        mask(1)
         gather_v(0)
         scale_and_mask(0)
         scale_and_mask(1)
@@ -242,14 +246,14 @@ def tile_attend_x_ks_draft_kernel(tc, qT, kT, vT, ks, vs, pos, qpos, offs, out):
         row_max(0)
         row_max(1)
         turn_v(0, 0)
-        turn_v(0, 1)
         exponent(0)
+        turn_v(0, 1)
         exponent(1)
         turn_prob(0)
         weights(0)
         turn_v(1, 0)
-        turn_v(1, 1)
         turn_prob(1)
+        turn_v(1, 1)
         quantize_w(0)
         weights(1)
         nc.vector.reciprocal(inv[0][:], total[0][:])

from contextlib import ExitStack

import concourse.mybir as mybir
from concourse.masks import make_identity

F32 = mybir.dt.float32
BF16 = mybir.dt.bfloat16
U32 = mybir.dt.uint32
U16 = mybir.dt.uint16
U8 = mybir.dt.uint8
FP8X4 = mybir.dt.float8_e4m3fn_x4
ALU = mybir.AluOpType
ACT = mybir.ActivationFunctionType
AXIS_X = mybir.AxisListType.X

B, NQ, D, DV, N, T = 2, 128, 512, 256, 512, 2048
P = 128
PACK = 4
CHUNKS = N // P
E_BLOCKS = DV // P
MASKED = 1.0e30
VECTOR_COLS = 256

FLOPS = 2 * B * NQ * N * (D + DV)
BYTES = 4 * (B * D * NQ + (D + DV) * T + 3 * T + B * NQ + B * NQ * DV) + 2 * P * (B * N // 16)


def tile_attend_x_ks_draft_kernel(tc, qT, kT, vT, ks, vs, pos, qpos, offs, out):
    nc = tc.nc
    with ExitStack() as ctx:
        keep = ctx.enter_context(tc.tile_pool(name="keep", bufs=1))
        psum = ctx.enter_context(tc.psum_pool(name="psum", bufs=8))

        def bank():
            return psum.tile([P, 512], F32, name="bank")

        def per_seq(shape, dtype, name, align=32):
            return [keep.tile(shape, dtype, name=f"{name}{s}", align_bytes=align) for s in range(B)]

        def seq(s):
            return slice(s * N, (s + 1) * N)

        offsets = keep.tile([P, B * N // 16], U16, name="offsets")
        nc.sync.dma_start(offsets[:], offs)
        table = {}
        for name, src, engine in (("pos", pos, nc.vector), ("ks", ks, nc.gpsimd), ("vs", vs, nc.vector)):
            table[name] = keep.tile([P, T], F32, name=name + "_table")
            engine.memset(table[name][:], 0.0)
            nc.scalar.dma_start(table[name][0:1, :], src[0:1, :])
        q_place = per_seq([P, 1], F32, "q_place")
        for s in range(B):
            nc.scalar.dma_start(q_place[s][:], qpos[s])
        k_rows = kT.rearrange("(p t) n -> p t n", t=PACK)
        k_pool = [keep.tile([P, T], F32, name=f"k_pool{t}") for t in range(PACK)]
        v_pool = [keep.tile([P, T], F32, name=f"v_pool{e}") for e in range(E_BLOCKS)]
        q_raw = keep.tile([P, B, PACK, NQ], F32, name="q_raw")
        nc.sync.dma_start(k_pool[0][:], k_rows[:, 0, :])
        nc.sync.dma_start(k_pool[1][:], k_rows[:, 1, :])
        nc.sync.dma_start(q_raw[:], qT.rearrange("b (p t) q -> p b t q", t=PACK))
        nc.sync.dma_start(k_pool[2][:], k_rows[:, 2, :])
        nc.sync.dma_start(k_pool[3][:], k_rows[:, 3, :])
        for e in range(E_BLOCKS):
            nc.sync.dma_start(v_pool[e][:], vT[e * P : (e + 1) * P, :])

        ident = keep.tile([P, P], F32, name="ident")
        make_identity(nc, ident[:])
        warm = keep.tile([P, 1], F32, name="warm")
        nc.vector.memset(warm[:], 0.0)
        nc.scalar.activation(warm[:], warm[:], ACT.Exp)

        q_row = keep.tile([P, B, NQ], F32, name="q_row")
        ps = bank()
        for s in range(B):
            nc.tensor.transpose(ps[:, s * NQ : (s + 1) * NQ], q_place[s][:].to_broadcast([P, P]), ident[:])
        nc.scalar.copy(out=q_row[:].rearrange("p b q -> p (b q)"), in_=ps[:, 0 : B * NQ])

        def gather_table(name):
            got = keep.tile([P, B * N], F32, name=name + "_got")
            nc.vector.tensor_copy(got[:], table[name][:].indirect(offsets[:]))
            return got

        def turn_table(name, got, start, step, scale):
            col = per_seq([P, CHUNKS], F32, name + "_col")
            for s in range(B):
                ps = bank()
                for c in range(CHUNKS):
                    a = s * N + c * start
                    nc.tensor.transpose(ps[:, c * P : (c + 1) * P], got[:, a : a + (P - 1) * step + 1 : step], ident[:])
                nc.scalar.activation(col[s][:], ps[:, 0 : 512 : P], ACT.Copy, scale=scale)
            return col

        pos_col = turn_table("pos", gather_table("pos"), P, 1, 1.0)
        limit = per_seq([P, CHUNKS, NQ], F32, "limit")

        def mask(s):
            for c in range(CHUNKS):
                nc.vector.tensor_scalar(
                    limit[s][:, c, :], q_row[:, s, :], pos_col[s][:, c : c + 1], MASKED, ALU.is_lt, ALU.mult
                )

        nks_col = turn_table("ks", gather_table("ks"), P, 1, -1.0)

        k_got = keep.tile([P, PACK, B * N], F32, name="k_got")
        k_bf = per_seq([P, N, PACK], BF16, "k_bf", 64)
        k_codes = per_seq([P, N], U32, "k_codes", 64)
        k_scales = per_seq([P, N], U8, "k_scales", 64)

        def gather_k(t):
            nc.vector.tensor_copy(k_got[:, t, :], k_pool[t][:].indirect(offsets[:]))

        def gather_last_k(s):
            list_s = offsets[:, s * (N // 16) : (s + 1) * (N // 16)]
            nc.vector.tensor_copy(k_got[:, 3, seq(s)], k_pool[3][:].indirect(list_s))

        def interleave(copy, s, t, a, z):
            copy(out=k_bf[s][:, a:z, t : t + 2], in_=k_got[:, t : t + 2, s * N + a : s * N + z].rearrange("p t n -> p n t"))

        def quantize_k(s):
            nc.vector.quantize_mx(
                out=k_codes[s][:].bitcast(FP8X4), scales=k_scales[s][:], in_=k_bf[s][:].rearrange("p n t -> p (n t)")
            )

        gather_k(0)
        vs_col = turn_table("vs", gather_table("vs"), 1, PACK, 1.0)
        gather_k(1)

        q_bf = keep.tile([P, B, NQ, PACK], BF16, name="q_bf", align_bytes=64)
        nc.scalar.copy(out=q_bf[:], in_=q_raw[:].rearrange("p b t q -> p b q t"))
        q_codes = keep.tile([P, B * NQ], U32, name="q_codes", align_bytes=64)
        q_scales = keep.tile([P, B * NQ], U8, name="q_scales", align_bytes=64)
        nc.vector.quantize_mx(
            out=q_codes[:].bitcast(FP8X4), scales=q_scales[:], in_=q_bf[:].rearrange("p b q t -> p (b q t)")
        )
        for s in range(B):
            interleave(nc.scalar.copy, s, 0, 0, N)
        gather_k(2)

        scaled = per_seq([P, CHUNKS, NQ], F32, "scaled")
        negmax = per_seq([P, 1], F32, "negmax")
        total = per_seq([P, 1], F32, "total")
        inv = per_seq([P, 1], F32, "inv")
        prob = per_seq([P, PACK, P], F32, "prob")
        w_bf = per_seq([P, NQ, PACK], BF16, "w_bf", 64)
        w_codes = per_seq([P, NQ], U32, "w_codes", 64)
        w_scales = per_seq([P, NQ], U8, "w_scales", 64)
        v_got = [keep.tile([P, B * N], F32, name=f"v_got{e}") for e in range(E_BLOCKS)]
        v_bf = per_seq([P, DV, PACK], BF16, "v_bf", 64)
        v_codes = per_seq([P, DV], U32, "v_codes", 64)
        v_scales = per_seq([P, DV], U8, "v_scales", 64)
        result = per_seq([P, DV], F32, "result")
        turned = {}

        def scores(s):
            ps = bank()
            qc = slice(s * NQ, (s + 1) * NQ)
            for c in range(CHUNKS):
                kc = slice(c * P, (c + 1) * P)
                nc.tensor.matmul_mx(
                    out=ps[:, kc], lhsT=k_codes[s][:, kc].bitcast(FP8X4), lhsT_scale=k_scales[s][:, kc],
                    rhs=q_codes[:, qc].bitcast(FP8X4), rhs_scale=q_scales[:, qc], start=True, stop=True,
                )
            turned["raw", s] = ps

        def scale_and_mask(s):
            ps = turned["raw", s]
            for c in range(CHUNKS):
                nc.scalar.activation(
                    scaled[s][:, c, :], ps[:, c * P : (c + 1) * P], ACT.Copy, scale=nks_col[s][:, c : c + 1]
                )

        def turn_scores(s):
            ps = bank()
            for c in range(CHUNKS):
                kc = slice(c * P, (c + 1) * P)
                nc.tensor.matmul(ps[:, kc], limit[s][:, c, :], ident[:], is_transpose=True, start=True, stop=False)
                nc.tensor.matmul(ps[:, kc], scaled[s][:, c, :], ident[:], is_transpose=True, start=False, stop=True)
            turned["score", s] = ps

        def row_max(s):
            nc.vector.tensor_reduce(negmax[s][:], turned["score", s][:], AXIS_X, ALU.min)

        def exponent(s):
            nc.scalar.activation(
                prob[s][:].rearrange("q t i -> q i t"), turned["score", s][:].rearrange("q (i t) -> q i t", t=PACK),
                ACT.Exp, bias=negmax[s][:], scale=-1.0, accum_out=total[s][:],
            )

        def turn_prob(s):
            ps = bank()
            for t in range(PACK):
                nc.tensor.transpose(ps[:, t * P : (t + 1) * P], prob[s][:, t, :], ident[:])
            turned["prob", s] = ps

        def weights(s):
            nc.vector.tensor_tensor(
                w_bf[s][:], turned["prob", s][:].rearrange("p (t q) -> p q t", t=PACK),
                vs_col[s][:].unsqueeze(1).to_broadcast([P, NQ, PACK]), ALU.mult,
            )

        def quantize_w(s):
            nc.vector.quantize_mx(
                out=w_codes[s][:].bitcast(FP8X4), scales=w_scales[s][:], in_=w_bf[s][:].rearrange("p q t -> p (q t)")
            )

        def gather_v(e):
            nc.vector.tensor_copy(v_got[e][:], v_pool[e][:].indirect(offsets[:]))

        def turn_v(e, s):
            ps = bank()
            for t in range(PACK):
                nc.tensor.transpose(ps[:, t * P : (t + 1) * P], v_got[e][:, s * N + t : (s + 1) * N : PACK], ident[:])
            nc.scalar.copy(out=v_bf[s][:, e * P : (e + 1) * P, :], in_=ps[:].rearrange("p (t c) -> p c t", t=PACK))

        def quantize_v(s):
            nc.vector.quantize_mx(
                out=v_codes[s][:].bitcast(FP8X4), scales=v_scales[s][:], in_=v_bf[s][:].rearrange("p c t -> p (c t)")
            )

        def values(s):
            ps = bank()
            nc.tensor.matmul_mx(
                out=ps[:, 0:DV], lhsT=w_codes[s][:].bitcast(FP8X4), lhsT_scale=w_scales[s][:],
                rhs=v_codes[s][:].bitcast(FP8X4), rhs_scale=v_scales[s][:], start=True, stop=True,
            )
            nc.scalar.activation(result[s][:], ps[:, 0:DV], ACT.Copy, scale=inv[s][:])
            nc.sync.dma_start(out[s], result[s][:])

        gather_last_k(0)
        interleave(nc.scalar.copy, 0, 2, VECTOR_COLS, N)
        gather_last_k(1)
        interleave(nc.vector.tensor_copy, 0, 2, 0, VECTOR_COLS)
        interleave(nc.scalar.copy, 1, 2, VECTOR_COLS, N)
        interleave(nc.vector.tensor_copy, 1, 2, 0, VECTOR_COLS)
        quantize_k(0)
        quantize_k(1)
        scores(0)
        scores(1)
        mask(0)
        mask(1)
        gather_v(0)
        scale_and_mask(0)
        scale_and_mask(1)
        turn_scores(0)
        turn_scores(1)
        gather_v(1)
        row_max(0)
        row_max(1)
        turn_v(0, 0)
        exponent(0)
        turn_v(0, 1)
        exponent(1)
        turn_prob(0)
        weights(0)
        turn_v(1, 0)
        turn_prob(1)
        turn_v(1, 1)
        quantize_w(0)
        weights(1)
        nc.vector.reciprocal(inv[0][:], total[0][:])
        nc.vector.reciprocal(inv[1][:], total[1][:])
        quantize_v(0)
        values(0)
        quantize_w(1)
        quantize_v(1)
        values(1)
